import numpy as np
import ml_dtypes


def mxq(x, axis, fmt="e4m3"):
    dtype, down = {"e4m3": (ml_dtypes.float8_e4m3fn, 7), "e5m2": (ml_dtypes.float8_e5m2, 14)}[fmt]
    v = np.moveaxis(np.asarray(x, np.float32).astype(ml_dtypes.bfloat16).astype(np.float64), axis, -1)
    blocks = v.reshape(v.shape[:-1] + (-1, 32))
    amax = np.abs(blocks).max(-1, keepdims=True)
    byte = np.maximum(np.where(amax > 0, np.frexp(amax)[1] - 1 + 127, 0) - down, 1)
    scale = np.exp2(byte - 127.0)
    codes = (blocks / scale).astype(np.float32).astype(dtype).astype(np.float64)
    return np.moveaxis((codes * scale).reshape(v.shape), -1, axis)


WIDE = False


def mx_kscale(k):
    if not WIDE:
        return np.ones(k)
    levels = np.array([10, -10, 5, -5, 0])
    if k % 512:
        return np.exp2(np.random.permutation(np.resize(levels, k // 32))).repeat(32)
    a = np.empty((k // 512, 16))
    for p in range(k // 512):
        a[p, :8] = np.random.permutation(np.resize(levels, 8))
        for g in range(8):
            far = levels[np.abs(levels - a[p, g]) >= 10]
            a[p, g + 8] = far[np.random.randint(len(far))]
    return np.exp2(a.ravel()).repeat(32)


BF16 = ml_dtypes.bfloat16


def bf(x):
    return np.asarray(x, np.float32).astype(BF16)


def f64(x):
    return np.asarray(x).astype(np.float64)

def planes(Y):
    n, m = Y.shape
    b = f64(bf(Y)).reshape(n // 32, 32, m)
    amax = np.abs(b).max(1)
    byte = np.clip(np.where(amax > 0, np.frexp(amax)[1] - 1 + 127 - 7, 1), 1, 254)
    codes = (b * np.exp2(127.0 - byte)[:, None, :]).reshape(n, m).astype(np.float32).astype(ml_dtypes.float8_e4m3fn).view(np.uint8)
    words = codes.reshape(n // 512, 128, 4, m).transpose(0, 1, 3, 2)
    return np.ascontiguousarray(words), np.ascontiguousarray(byte.astype(np.uint8).reshape(n // 512, 16, m))


N, D, F, E, O = 1024, 512, 1024, 4, 512


def setup_inputs():
    s, t = mx_kscale(D), mx_kscale(F)
    scale_d = 1.5 / np.sqrt(D)
    scale_g2 = 2.0 / np.sqrt(F)
    scale_f = 1.5 / np.sqrt(F)
    return {
        "x": bf(np.random.standard_normal((N, D)) * s),
        "wg1": bf(np.random.standard_normal((D, E)) * scale_d / s[:, None]),
        "w1": bf(np.random.standard_normal((E, D, F)) * scale_d / s[None, :, None]),
        "b1": bf(np.random.standard_normal((E, F)) * 0.3),
        "wg2": bf(np.random.standard_normal((F, E)) * scale_g2),
        "gamma": bf(np.random.standard_normal(F) * t),
        "w2": bf(np.random.standard_normal((E, F, O)) * scale_f / t[None, :, None]),
    }


def gate(inp, wg):
    logits = np.sum(inp[:, :, None] * wg[None, :, :], axis=1)
    e = np.exp(logits - logits.max(-1, keepdims=True))
    return e / e.sum(-1, keepdims=True)


def mix(g, h):
    return np.sum(g.T[:, :, None] * h, axis=0)


def core(x, wg1, w1, b1, wg2, gamma, w2):
    g1 = gate(f64(x), f64(wg1))
    xq = mxq(f64(x), 1, "e4m3")
    h = np.maximum((xq[None, :, :] @ mxq(f64(w1), 1, "e4m3")) + f64(b1)[:, None, :], 0.0)
    z1 = mix(g1, h)
    g2 = gate(z1, f64(wg2))
    u = z1 * f64(gamma)[None, :]
    uq = mxq(u, 1, "e4m3")
    q = np.maximum(uq[None, :, :] @ mxq(f64(w2), 1, "e4m3"), 0.0)
    return mix(g2, q)


def reference(x, wg1, w1, b1, wg2, gamma, w2):
    R_out = core(x, wg1, w1, b1, wg2, gamma, w2)
    words, scales = planes(R_out.T)
    return R_out, words, scales

@@ -1,0 +1,506 @@
+from contextlib import ExitStack
+
+import concourse.mybir as mybir
+from concourse.masks import make_identity
+
+N, D, F, E, O = 1024, 512, 1024, 4, 512
+FLOPS = 2 * N * D * F * E + 2 * N * F * O * E
+
+F32 = mybir.dt.float32
+BF16 = mybir.dt.bfloat16
+U32 = mybir.dt.uint32
+I32 = mybir.dt.int32
+U8 = mybir.dt.uint8
+X4 = mybir.dt.float8_e4m3fn_x4
+ADD = mybir.AluOpType.add
+SUB = mybir.AluOpType.subtract
+MUL = mybir.AluOpType.mult
+MAX = mybir.AluOpType.max
+AX = mybir.AxisListType.X
+ACT = mybir.ActivationFunctionType
+
+P = 128
+T = 4
+G = 2
+NT = N // P
+
+GPS = (1, 3)
+R2 = 'sv'
+A2 = 'ggvg'
+HC = 208
+prep_at = {2: (4, 0), 3: (5, 0), 4: (6, 0), 5: (7, 0), 7: (8, 0), 9: (9, 0), 11: (10, 0), 13: (11, 0), 15: (12, 128), 16: (13, 256), 17: (14, 256), 18: (15, 256)}
+quant_at = {4: 4, 5: 5, 6: 6, 7: 7, 9: 8, 11: 9, 13: 10, 15: 11, 16: 12, 17: 13, 18: 14, 19: 15}
+units_at = {
+    15: [(0, 0), (0, 1)],
+    16: [(1, 0), (1, 1)],
+    17: [(0, 2), (0, 3), (1, 2), (1, 3)],
+    18: [(2, 0), (2, 1), (2, 2), (2, 3)],
+    19: [(0, 4), (0, 5), (1, 4), (1, 5), (2, 4), (2, 5)],
+}
+tail = [(e, i) for e in range(3) for i in (6, 7)] + [(3, i) for i in range(8)]
+prep_tail = {}
+
+
+def tile_stackeddeepmixtureofexperts_x1_kernel(tc, x, wg1, w1, b1, wg2, gamma, w2, out_0, out_1, out_2):
+    nc = tc.nc
+    with ExitStack() as ctx:
+        keep = ctx.enter_context(tc.tile_pool(name="keep", bufs=1))
+        work = ctx.enter_context(tc.tile_pool(name="work", bufs=3))
+        mmp = ctx.enter_context(tc.psum_pool(name="mmp", bufs=5))
+        zp = ctx.enter_context(tc.psum_pool(name="zp", bufs=2))
+        mp = ctx.enter_context(tc.psum_pool(name="mp", bufs=1))
+
+        ident = keep.tile([P, P], F32, name="ident", align_bytes=64)
+        wg1_sb = keep.tile([P, T, E], BF16, name="wg1_sb", align_bytes=64)
+        wg2_bf = keep.tile([P, G, T, E], BF16, name="wg2_bf", align_bytes=64)
+        wg2_sb = keep.tile([P, G, T, E], F32, name="wg2_sb", align_bytes=64)
+        gam = keep.tile([P, G, T], BF16, name="gam", align_bytes=64)
+        b_raw = [keep.tile([P, E, 512], BF16, name=f"b_raw{g}", align_bytes=64) for g in range(G)]
+        b_perm = [keep.tile([P, E, T, P], BF16, name=f"b_perm{g}", align_bytes=64) for g in range(G)]
+        x_sb = [keep.tile([P, 2, D], BF16, name=f"x_sb{j}", align_bytes=64) for j in range(4)]
+        xg = [keep.tile([P, 256, T], BF16, name=f"xg{j}", align_bytes=64) for j in range(4)]
+        xc = [keep.tile([P, 256], U32, name=f"xc{j}", align_bytes=64) for j in range(4)]
+        xs = [keep.tile([P, 256], U8, name=f"xs{j}", align_bytes=64) for j in range(4)]
+        g1 = [keep.tile([P, 2, E], F32, name=f"g1_{j}", align_bytes=64) for j in range(4)]
+        g2 = [keep.tile([P, 2, E], F32, name=f"g2_{j}", align_bytes=64) for j in range(4)]
+        uc = [[keep.tile([P, P], U32, name=f"uc{g}_{i}", align_bytes=64) for i in range(NT)] for g in range(G)]
+        us = [[keep.tile([P, P], U8, name=f"us{g}_{i}", align_bytes=64) for i in range(NT)] for g in range(G)]
+        acc = [keep.tile([P, O], F32, name=f"acc{i}", align_bytes=64) for i in range(NT)]
+        oc = [keep.tile([P, 512], U32, name=f"oc{h}", align_bytes=64) for h in range(2)]
+        osc = [keep.tile([P, 512], U8, name=f"osc{h}", align_bytes=64) for h in range(2)]
+        warm = keep.tile([P, 1], F32, name="warm")
+
+        w_codes = {}
+        w_scales = {}
+        for s in range(2):
+            for g in range(G):
+                for e in range(E):
+                    w_codes[s, g, e] = keep.tile([P, 512], U32, name=f"wc{s}_{g}_{e}", align_bytes=64)
+                    w_scales[s, g, e] = keep.tile([P, 512], U8, name=f"ws{s}_{g}_{e}", align_bytes=64)
+
+        lgs = mp.tile([P, 2, NT, E], F32, name="lgs")
+
+        pieces = [(0, 0, e) for e in range(E)] + [(0, 1, e) for e in range(E)]
+        pieces += [(1, g, e) for e in range(E) for g in range(G)]
+
+        raw = {}
+        grouped = {}
+
+        def load_piece(pc):
+            s, g, e = pc
+            w_raw = work.tile([P, T, 512], BF16, name="w_raw", bufs=8, align_bytes=64)
+            if s == 0:
+                src = w1[e, :, 512 * g : 512 * (g + 1)]
+            else:
+                src = w2[e, 512 * g : 512 * (g + 1), :]
+            nc.sync.dma_start(out=w_raw[:], in_=src.rearrange("(p j) c -> p j c", j=T))
+            raw[pc] = w_raw
+
+        def prep_copy(pc, c):
+            w_grp = work.tile([P, 512, T], BF16, name="w_grp", bufs=3, align_bytes=64)
+            grouped[pc] = w_grp
+            if c > 0:
+                nc.vector.tensor_copy(out=w_grp[:, :c, :], in_=raw[pc][:, :, :c].rearrange("p j c -> p c j"))
+            if c < 512:
+                nc.scalar.copy(out=w_grp[:, c:, :], in_=raw[pc][:, :, c:].rearrange("p j c -> p c j"))
+
+        def prep_quant(pc):
+            nc.vector.quantize_mx(
+                out=w_codes[pc][:].bitcast(X4),
+                scales=w_scales[pc][:],
+                in_=grouped[pc][:].rearrange("p c j -> p (c j)"),
+            )
+
+        def x_turn(j):
+            xt = mmp.tile([P, 2, 2, P], F32, name="ps")
+            for i in range(2):
+                words = x_sb[j][:, i, :].bitcast(F32)
+                for u in range(2):
+                    nc.tensor.transpose(xt[:, i, u, :], words[:, u:256:2], ident[:])
+            return xt
+
+        def x_copy(j, xt, eng):
+            dst = xg[j][:].rearrange("p n t -> p (n t)").bitcast(F32).rearrange("p (i r u) -> p i r u", i=2, u=2)
+            src = xt[:].rearrange("p i u r -> p i r u")
+            if eng == "v":
+                nc.vector.tensor_copy(out=dst, in_=src)
+            else:
+                nc.scalar.copy(out=dst, in_=src)
+
+        def x_quant(j):
+            nc.vector.quantize_mx(out=xc[j][:].bitcast(X4), scales=xs[j][:], in_=xg[j][:].rearrange("p n t -> p (n t)"))
+
+        def logits1(j):
+            lg = lgs[:, 0, 2 * j : 2 * j + 2, :]
+            for i in range(2):
+                for t in range(T):
+                    nc.tensor.matmul(
+                        out=lg[:, i, :],
+                        lhsT=xg[j][:, P * i : P * (i + 1), t],
+                        rhs=wg1_sb[:, t, :],
+                        start=(t == 0),
+                        stop=(t == T - 1),
+                    )
+            return lg
+
+        def softmax_ops(lg, gt):
+            mx = work.tile([P, 2], F32, name="mx", align_bytes=64)
+            dl = work.tile([P, 2, E], F32, name="dl", align_bytes=64)
+            ex = work.tile([P, 2, E], F32, name="ex", align_bytes=64)
+            sm = work.tile([P, 2], F32, name="sm", align_bytes=64)
+            rc = work.tile([P, 2], F32, name="rc", align_bytes=64)
+
+            def top():
+                nc.vector.tensor_reduce(out=mx[:], in_=lg, axis=AX, op=MAX)
+
+            def exps():
+                nc.vector.tensor_tensor(out=dl[:], in0=lg, in1=mx[:].unsqueeze(2).to_broadcast([P, 2, E]), op=SUB)
+                nc.scalar.activation(out=ex[:], in_=dl[:], func=ACT.Exp)
+
+            def total():
+                nc.vector.tensor_reduce(out=sm[:], in_=ex[:], axis=AX, op=ADD)
+
+            def inverse():
+                nc.vector.reciprocal(out=rc[:], in_=sm[:])
+
+            def gates():
+                nc.vector.tensor_tensor(out=gt[:], in0=ex[:], in1=rc[:].unsqueeze(2).to_broadcast([P, 2, E]), op=MUL)
+
+            return [top, exps, total, inverse, gates]
+
+        ps1 = {}
+        tt1 = {}
+        r1 = {}
+        zps = {}
+        z1 = {}
+        ub = {}
+
+        def mm1(k, e):
+            g, i = divmod(k, NT)
+            cols = slice(P * (i % 2), P * (i % 2 + 1))
+            ps = mmp.tile([P, 512], F32, name="ps")
+            nc.tensor.matmul_mx(
+                out=ps[:],
+                lhsT=xc[i // 2][:, cols].bitcast(X4),
+                lhsT_scale=xs[i // 2][:, cols],
+                rhs=w_codes[0, g, e][:].bitcast(X4),
+                rhs_scale=w_scales[0, g, e][:],
+                start=True,
+                stop=True,
+            )
+            ps1[k, e] = ps
+
+        def add1(k, e):
+            tt = work.tile([P, T, P], F32, name="tt", bufs=4, align_bytes=64)
+            nc.vector.tensor_tensor(
+                out=tt[:], in0=ps1[k, e][:].rearrange("p (m t) -> p t m", t=T), in1=b_perm[k // NT][:, e], op=ADD
+            )
+            tt1[k, e] = tt
+
+        def relu1(k, e, eng="s"):
+            i = k % NT
+            r = work.tile([P, T, P], F32, name="r", bufs=12, align_bytes=64)
+            gate = g1[i // 2][:, i % 2, e : e + 1]
+            if eng == "s":
+                nc.scalar.activation(out=r[:], in_=tt1[k, e][:], func=ACT.Relu, scale=gate)
+            else:
+                nc.gpsimd.tensor_scalar(out=r[:], in0=tt1[k, e][:], scalar1=gate, scalar2=0.0, op0=MUL, op1=MAX)
+            r1[k, e] = r
+
+        def turn1(k):
+            z = zp.tile([P, T, P], F32, name="z")
+            for t in range(T):
+                for e in range(E):
+                    nc.tensor.matmul(
+                        out=z[:, t, :],
+                        lhsT=r1[k, e][:, t, :],
+                        rhs=ident[:],
+                        is_transpose=True,
+                        start=(e == 0),
+                        stop=(e == E - 1),
+                    )
+            zps[k] = z
+
+        def z_copy(k):
+            zz = work.tile([P, T, P], F32, name="z1", bufs=11, align_bytes=64)
+            nc.scalar.copy(out=zz[:], in_=zps[k][:])
+            z1[k] = zz
+
+        def u_mul(k):
+            g = k // NT
+            u = work.tile([P, P, T], BF16, name="ub", bufs=3, align_bytes=64)
+            nc.vector.tensor_tensor(
+                out=u[:],
+                in0=zps[k][:].rearrange("p t n -> p n t"),
+                in1=gam[:, g, :].unsqueeze(1).to_broadcast([P, P, T]),
+                op=MUL,
+            )
+            ub[k] = u
+
+        def u_quant(k):
+            g, i = divmod(k, NT)
+            nc.vector.quantize_mx(
+                out=uc[g][i][:].bitcast(X4), scales=us[g][i][:], in_=ub[k][:].rearrange("p n t -> p (n t)")
+            )
+
+        lg2 = {}
+
+        def logits2(i):
+            lg2[i // 2] = lgs[:, 1, i - i % 2 : i - i % 2 + 2, :]
+            for g in range(G):
+                for t in range(T):
+                    nc.tensor.matmul(
+                        out=lg2[i // 2][:, i % 2, :],
+                        lhsT=z1[NT * g + i][:, t, :],
+                        rhs=wg2_sb[:, g, t, :],
+                        start=(g == 0 and t == 0),
+                        stop=(g == G - 1 and t == T - 1),
+                    )
+
+        ps2 = {}
+        r2 = {}
+
+        def mm2(e, i):
+            q = mmp.tile([P, 512], F32, name="ps")
+            for g in range(G):
+                nc.tensor.matmul_mx(
+                    out=q[:],
+                    lhsT=uc[g][i][:].bitcast(X4),
+                    lhsT_scale=us[g][i][:],
+                    rhs=w_codes[1, g, e][:].bitcast(X4),
+                    rhs_scale=w_scales[1, g, e][:],
+                    start=(g == 0),
+                    stop=(g == G - 1),
+                )
+            ps2[e, i] = q
+
+        def relu2(e, i, eng):
+            gate = g2[i // 2][:, i % 2, e : e + 1]
+            if e == 0:
+                dst = acc[i]
+            else:
+                rr = work.tile([P, O], F32, name="rr", bufs=5, align_bytes=64)
+                dst = rr
+            r2[e, i] = dst
+            if eng == "s":
+                nc.scalar.activation(out=dst[:], in_=ps2[e, i][:], func=ACT.Relu, scale=gate)
+            else:
+                nc.vector.tensor_scalar(out=dst[:], in0=ps2[e, i][:], scalar1=gate, scalar2=0.0, op0=MUL, op1=MAX)
+
+        def add2(e, i, eng):
+            if e == 0:
+                return
+            e_ = nc.gpsimd if eng == "g" else nc.vector
+            e_.tensor_tensor(out=acc[i][:], in0=acc[i][:], in1=r2[e, i][:], op=ADD)
+
+        ot = {}
+        pb = {}
+
+        def out_turn(i):
+            nc.sync.dma_start(out=out_0[P * i : P * (i + 1), :], in_=acc[i][:])
+            z = zp.tile([P, T, P], F32, name="z")
+            for t in range(T):
+                nc.tensor.transpose(z[:, t, :], acc[i][:, t:O:T], ident[:])
+            ot[i] = z
+
+        def out_copy(i, eng):
+            b = work.tile([P, P, T], BF16, name="pb", bufs=3, align_bytes=64)
+            src = ot[i][:].rearrange("p t n -> p n t")
+            if eng == "s":
+                nc.scalar.copy(out=b[:], in_=src)
+            else:
+                nc.vector.tensor_copy(out=b[:], in_=src)
+            pb[i] = b
+
+        def out_quant(i):
+            h, c = divmod(i, 4)
+            cols = slice(P * c, P * (c + 1))
+            nc.vector.quantize_mx(
+                out=oc[h][:, cols].bitcast(X4), scales=osc[h][:, cols], in_=pb[i][:].rearrange("p n t -> p (n t)")
+            )
+
+        def out_store(h):
+            words = out_1[0].rearrange("p m t -> p (m t)")
+            nc.sync.dma_start(out=words[:, 2048 * h : 2048 * (h + 1)].bitcast(I32), in_=oc[h][:].bitcast(I32))
+            for q in range(4):
+                nc.sync.dma_start(
+                    out=out_2[0, 4 * q : 4 * q + 4, 512 * h : 512 * (h + 1)].bitcast(I32),
+                    in_=osc[h][32 * q : 32 * q + 4, :].bitcast(I32),
+                )
+
+        make_identity(nc, ident[:])
+        nc.gpsimd.memset(warm[:], 0.0)
+        nc.scalar.activation(out=warm[:], in_=warm[:], func=ACT.Exp)
+
+        def load_x(j):
+            nc.sync.dma_start(out=x_sb[j][:], in_=x[256 * j : 256 * (j + 1), :].rearrange("(i p) k -> p i k", p=P))
+
+        def load_bias(g):
+            nc.sync.dma_start(out=b_raw[g][:], in_=b1[:, 512 * g : 512 * (g + 1)].partition_broadcast(P))
+
+        def perm_bias(g):
+            for e in range(E):
+                nc.gpsimd.tensor_scalar(
+                    out=b_perm[g][:, e],
+                    in0=b_raw[g][:, e, :].rearrange("p (m t) -> p t m", t=T),
+                    scalar1=1.0,
+                    scalar2=0.0,
+                    op0=MUL,
+                    op1=ADD,
+                )
+
+        nc.sync.dma_start(out=wg1_sb[:], in_=wg1.rearrange("(p t) e -> p t e", t=T))
+        load_x(0)
+        load_piece(pieces[0])
+        load_bias(0)
+        load_piece(pieces[1])
+        load_piece(pieces[2])
+        load_x(1)
+        load_piece(pieces[3])
+        load_x(2)
+        nc.sync.dma_start(out=gam[:], in_=gamma.rearrange("(g p t) -> p g t", g=G, t=T))
+        load_x(3)
+        nc.sync.dma_start(out=wg2_bf[:], in_=wg2.rearrange("(g p t) e -> p g t e", g=G, t=T))
+        load_piece(pieces[4])
+        load_bias(1)
+        for pc in pieces[5:8]:
+            load_piece(pc)
+
+        with tc.manual_schedule():
+            perm_bias(0)
+
+            def x_a(j, eng):
+                xt = x_turn(j)
+                x_copy(j, xt, eng)
+
+            lg1 = {}
+
+            def relu_eng(k, e):
+                return "g" if e in GPS else "s"
+
+            x_a(0, "v")
+            lg1[0] = logits1(0)
+            prep_copy(pieces[0], HC)
+            x_quant(0)
+            so = softmax_ops(lg1[0], g1[0])
+            so[0]()
+            so[1]()
+            prep_copy(pieces[1], HC)
+            prep_quant(pieces[0])
+            so[2]()
+            so[3]()
+            so[4]()
+            for e in range(E):
+                mm1(0, e)
+                mm1(1, e)
+                if e + 2 < E:
+                    prep_copy(pieces[e + 2], HC)
+                add1(0, e)
+                relu1(0, e, relu_eng(0, e))
+                if e + 1 < E:
+                    prep_quant(pieces[e + 1])
+                add1(1, e)
+                relu1(1, e, relu_eng(1, e))
+                if e == 0:
+                    x_a(1, "v")
+                if e == 1:
+                    lg1[1] = logits1(1)
+                    x_quant(1)
+                    so = softmax_ops(lg1[1], g1[1])
+                if e == 2:
+                    so[0]()
+                    so[1]()
+            so[2]()
+            for e in range(E):
+                mm1(2, e)
+            turn1(0)
+            so[3]()
+            so[4]()
+            perm_bias(1)
+            nc.gpsimd.tensor_copy(out=wg2_sb[:], in_=wg2_bf[:])
+
+            state = {"loaded": 8}
+
+            def load_next():
+                if state["loaded"] < len(pieces):
+                    load_piece(pieces[state["loaded"]])
+                    state["loaded"] += 1
+
+            count = [0]
+
+            def unit(e, i):
+                n = count[0]
+                mm2(e, i)
+                relu2(e, i, R2[n % len(R2)])
+                count[0] += 1
+
+            def unit_add(e, i, n):
+                add2(e, i, A2[n % len(A2)])
+
+            smx = []
+            for k in range(2, 20):
+                slots = [[] for q in range(E)]
+                if k in (2, 4):
+                    j = k // 2 + 1
+                    slots[0].append(lambda: x_a(j, "s"))
+                    slots[2].append(lambda: (lg1.update({j: logits1(j)}), x_quant(j)))
+                if k in (3, 5):
+                    j = (k + 1) // 2
+                    smx += softmax_ops(lg1[j], g1[j])
+                if k >= 13 and k % 2 == 1:
+                    smx += softmax_ops(lg2[(k - 13) // 2], g2[(k - 13) // 2])
+                for q in range(E):
+                    if smx:
+                        slots[q].insert(0, smx.pop(0))
+                if k in (3, 5):
+                    slots[3].insert(1, smx.pop(0))
+                if k in quant_at:
+                    slots[1].append(lambda: prep_quant(pieces[quant_at[k]]))
+                if 0 <= k - 3 < 16:
+                    slots[0].append(lambda: u_quant(k - 3))
+                if k - 2 < 16:
+                    slots[2].append(lambda: (u_mul(k - 2), z_copy(k - 2)))
+                if k in prep_at:
+                    slots[3].append(lambda: (prep_copy(pieces[prep_at[k][0]], prep_at[k][1]), load_next()))
+                for e in range(E):
+                    if k < 16:
+                        add1(k, e)
+                        relu1(k, e, relu_eng(k, e))
+                    for fn in slots[e]:
+                        fn()
+                if k - 1 < 16:
+                    turn1(k - 1)
+                if k + 1 < 16:
+                    for e in range(E):
+                        mm1(k + 1, e)
+                if 10 <= k < 18:
+                    logits2(k - 10)
+                for e, i in units_at.get(k, []):
+                    n = count[0]
+                    unit(e, i)
+                    unit_add(e, i, n)
+            for fn in smx:
+                fn()
+
+            LG = 2
+            for n in range(len(tail) + 4 + LG):
+                if n in prep_tail:
+                    prep_copy(pieces[prep_tail[n][0]], prep_tail[n][1])
+                if n < len(tail):
+                    unit(*tail[n])
+                if n - 2 in prep_tail:
+                    prep_quant(pieces[prep_tail[n - 2][0]])
+                f0 = tail[n - 1] if 0 <= n - 1 < len(tail) else None
+                f1 = tail[n - 1 - LG] if 0 <= n - 1 - LG < len(tail) else (0, 0)
+                f2 = tail[n - 2 - LG] if 0 <= n - 2 - LG < len(tail) else (0, 0)
+                f3 = tail[n - 3 - LG] if 0 <= n - 3 - LG < len(tail) else (0, 0)
+                if f0 is not None:
+                    unit_add(*f0, n)
+                if f1[0] == E - 1:
+                    out_turn(f1[1])
+                if f2[0] == E - 1:
+                    out_copy(f2[1], "s" if f2[1] % 2 else "v")
+                if f3[0] == E - 1:
+                    out_quant(f3[1])
+                    if f3[1] % 4 == 3:
+                        out_store(f3[1] // 4)

@@ -24,11 +24,11 @@ T = 4
 G = 2
 NT = N // P
 
-GPS = (1, 3)
-R2 = 'sv'
-A2 = 'ggvg'
+GPS = ()
+R2 = 'ssv'
+A2 = 'gvv'
 HC = 208
-prep_at = {2: (4, 0), 3: (5, 0), 4: (6, 0), 5: (7, 0), 7: (8, 0), 9: (9, 0), 11: (10, 0), 13: (11, 0), 15: (12, 128), 16: (13, 256), 17: (14, 256), 18: (15, 256)}
+prep_at = {2: (4, 0, 0), 3: (5, 0, 0), 4: (6, 0, 0), 5: (7, 0, 0), 7: (8, 0, 0), 9: (9, 0, 0), 11: (10, 0, 0), 13: (11, 0, 0), 15: (12, 128), 16: (13, 256), 17: (14, 256), 18: (15, 256)}
 quant_at = {4: 4, 5: 5, 6: 6, 7: 7, 9: 8, 11: 9, 13: 10, 15: 11, 16: 12, 17: 13, 18: 14, 19: 15}
 units_at = {
     15: [(0, 0), (0, 1)],
@@ -96,13 +96,27 @@ def tile_stackeddeepmixtureofexperts_x1_kernel(tc, x, wg1, w1, b1, wg2, gamma, w
             nc.sync.dma_start(out=w_raw[:], in_=src.rearrange("(p j) c -> p j c", j=T))
             raw[pc] = w_raw
 
-        def prep_copy(pc, c):
+        def prep_copy_g(pc, c0, n):
+            for q in range(n):
+                a, b = c0 + (512 - c0) * q // n, c0 + (512 - c0) * (q + 1) // n
+                nc.gpsimd.tensor_scalar(
+                    out=grouped[pc][:, a:b, :],
+                    in0=raw[pc][:, :, a:b].rearrange("p j c -> p c j"),
+                    scalar1=1.0,
+                    scalar2=0.0,
+                    op0=MUL,
+                    op1=ADD,
+                )
+
+        def prep_copy(pc, c, cg=512):
             w_grp = work.tile([P, 512, T], BF16, name="w_grp", bufs=3, align_bytes=64)
             grouped[pc] = w_grp
+            if cg < 512:
+                prep_copy_g(pc, cg, 4)
             if c > 0:
                 nc.vector.tensor_copy(out=w_grp[:, :c, :], in_=raw[pc][:, :, :c].rearrange("p j c -> p c j"))
-            if c < 512:
-                nc.scalar.copy(out=w_grp[:, c:, :], in_=raw[pc][:, :, c:].rearrange("p j c -> p c j"))
+            if c < cg:
+                nc.scalar.copy(out=w_grp[:, c:cg, :], in_=raw[pc][:, :, c:cg].rearrange("p j c -> p c j"))
 
         def prep_quant(pc):
             nc.vector.quantize_mx(
@@ -366,7 +380,7 @@ def tile_stackeddeepmixtureofexperts_x1_kernel(tc, x, wg1, w1, b1, wg2, gamma, w
         for pc in pieces[5:8]:
             load_piece(pc)
 
-        with tc.manual_schedule():
+        for once in range(1):
             perm_bias(0)
 
             def x_a(j, eng):
@@ -461,7 +475,7 @@ def tile_stackeddeepmixtureofexperts_x1_kernel(tc, x, wg1, w1, b1, wg2, gamma, w
                 if k - 2 < 16:
                     slots[2].append(lambda: (u_mul(k - 2), z_copy(k - 2)))
                 if k in prep_at:
-                    slots[3].append(lambda: (prep_copy(pieces[prep_at[k][0]], prep_at[k][1]), load_next()))
+                    slots[3].append(lambda: (prep_copy(pieces[prep_at[k][0]], *prep_at[k][1:]), load_next()))
                 for e in range(E):
                     if k < 16:
                         add1(k, e)

@@ -24,21 +24,28 @@ T = 4
 G = 2
 NT = N // P
 
-GPS = ()
-R2 = 'ssv'
-A2 = 'gvv'
+LOADS = [['x', 0], ['w', 0], ['b', 0], ['w', 1], ['w', 2], ['w', 3], ['x', 1], ['g', 0], ['x', 2], ['x', 3], ['h', 0], ['w', 4], ['b', 1], ['w', 5], ['w', 6], ['w', 7]]
+UG = [0]
+PEO = [0, 1, 4, 2, 3]
+LW = 64
 HC = 208
-prep_at = {2: (4, 0, 0), 3: (5, 0, 0), 4: (6, 0, 0), 5: (7, 0, 0), 7: (8, 0, 0), 9: (9, 0, 0), 11: (10, 0, 0), 13: (11, 0, 0), 15: (12, 128), 16: (13, 256), 17: (14, 256), 18: (15, 256)}
-quant_at = {4: 4, 5: 5, 6: 6, 7: 7, 9: 8, 11: 9, 13: 10, 15: 11, 16: 12, 17: 13, 18: 14, 19: 15}
-units_at = {
-    15: [(0, 0), (0, 1)],
-    16: [(1, 0), (1, 1)],
-    17: [(0, 2), (0, 3), (1, 2), (1, 3)],
-    18: [(2, 0), (2, 1), (2, 2), (2, 3)],
-    19: [(0, 4), (0, 5), (1, 4), (1, 5), (2, 4), (2, 5)],
-}
-tail = [(e, i) for e in range(3) for i in (6, 7)] + [(3, i) for i in range(8)]
+LG = 3
+GPS = ()
+PA = (1, 3)
+TE = (0, 2)
+R2 = 'sssv'
+A2 = 'vg'
+OC = 'vs'
+XE = 'vvss'
+RB = 16
+MB = 4
+ZB = 3
+seq = [0, 1, 2, 3, 4, 5, 6, 7, 8, 9, 10, 11, 12, 13, 14, 15]
+prep_at = {2: [(4, 128, 384)], 3: [(5, 128, 256)], 4: [(6, 128, 512)], 5: [(7, 128, 512)], 6: [(8, 384, 384)], 9: [(9, 256, 512), (10, 0, 256)], 12: [(11, 128, 128)], 13: [(12, 128, 512)], 15: [(13, 512, 512)], 16: [(14, 192, 512)], 17: [(15, 192, 256)]}
+quant_at = {3: [4], 4: [5], 5: [6], 6: [7], 7: [8], 10: [9], 11: [10], 14: [11, 12], 16: [13], 18: [14, 15]}
 prep_tail = {}
+quant_tail = {}
+UPP = [0, 0, 0, 0, 0, 0, 0, 0, 0, 0, 0, 2, 2, 0, 4, 0, 2, 3, 4]
 
 
 def tile_stackeddeepmixtureofexperts_x1_kernel(tc, x, wg1, w1, b1, wg2, gamma, w2, out_0, out_1, out_2):
@@ -46,14 +53,14 @@ def tile_stackeddeepmixtureofexperts_x1_kernel(tc, x, wg1, w1, b1, wg2, gamma, w
     with ExitStack() as ctx:
         keep = ctx.enter_context(tc.tile_pool(name="keep", bufs=1))
         work = ctx.enter_context(tc.tile_pool(name="work", bufs=3))
-        mmp = ctx.enter_context(tc.psum_pool(name="mmp", bufs=5))
-        zp = ctx.enter_context(tc.psum_pool(name="zp", bufs=2))
+        mmp = ctx.enter_context(tc.psum_pool(name="mmp", bufs=MB))
+        zp = ctx.enter_context(tc.psum_pool(name="zp", bufs=ZB))
         mp = ctx.enter_context(tc.psum_pool(name="mp", bufs=1))
 
         ident = keep.tile([P, P], F32, name="ident", align_bytes=64)
         wg1_sb = keep.tile([P, T, E], BF16, name="wg1_sb", align_bytes=64)
         wg2_bf = keep.tile([P, G, T, E], BF16, name="wg2_bf", align_bytes=64)
-        wg2_sb = keep.tile([P, G, T, E], F32, name="wg2_sb", align_bytes=64)
+        wg2_sb = keep.tile([P, G, T, LW], F32, name="wg2_sb", align_bytes=64)
         gam = keep.tile([P, G, T], BF16, name="gam", align_bytes=64)
         b_raw = [keep.tile([P, E, 512], BF16, name=f"b_raw{g}", align_bytes=64) for g in range(G)]
         b_perm = [keep.tile([P, E, T, P], BF16, name=f"b_perm{g}", align_bytes=64) for g in range(G)]
@@ -78,7 +85,9 @@ def tile_stackeddeepmixtureofexperts_x1_kernel(tc, x, wg1, w1, b1, wg2, gamma, w
                     w_codes[s, g, e] = keep.tile([P, 512], U32, name=f"wc{s}_{g}_{e}", align_bytes=64)
                     w_scales[s, g, e] = keep.tile([P, 512], U8, name=f"ws{s}_{g}_{e}", align_bytes=64)
 
-        lgs = mp.tile([P, 2, NT, E], F32, name="lgs")
+        lgs = mp.tile([P, NT * E + 4 * LW], F32, name="lgs")
+        lgs1 = lgs[:, : NT * E].rearrange("p (i e) -> p i e", e=E)
+        lgs2 = lgs[:, NT * E :].rearrange("p (i e) -> p i e", e=LW)
 
         pieces = [(0, 0, e) for e in range(E)] + [(0, 1, e) for e in range(E)]
         pieces += [(1, g, e) for e in range(E) for g in range(G)]
@@ -145,7 +154,7 @@ def tile_stackeddeepmixtureofexperts_x1_kernel(tc, x, wg1, w1, b1, wg2, gamma, w
             nc.vector.quantize_mx(out=xc[j][:].bitcast(X4), scales=xs[j][:], in_=xg[j][:].rearrange("p n t -> p (n t)"))
 
         def logits1(j):
-            lg = lgs[:, 0, 2 * j : 2 * j + 2, :]
+            lg = lgs1[:, 2 * j : 2 * j + 2, :]
             for i in range(2):
                 for t in range(T):
                     nc.tensor.matmul(
@@ -165,10 +174,10 @@ def tile_stackeddeepmixtureofexperts_x1_kernel(tc, x, wg1, w1, b1, wg2, gamma, w
             rc = work.tile([P, 2], F32, name="rc", align_bytes=64)
 
             def top():
-                nc.vector.tensor_reduce(out=mx[:], in_=lg, axis=AX, op=MAX)
+                nc.vector.tensor_reduce(out=mx[:], in_=lg[:, :, :E], axis=AX, op=MAX)
 
             def exps():
-                nc.vector.tensor_tensor(out=dl[:], in0=lg, in1=mx[:].unsqueeze(2).to_broadcast([P, 2, E]), op=SUB)
+                nc.vector.tensor_tensor(out=dl[:], in0=lg[:, :, :E], in1=mx[:].unsqueeze(2).to_broadcast([P, 2, E]), op=SUB)
                 nc.scalar.activation(out=ex[:], in_=dl[:], func=ACT.Exp)
 
             def total():
@@ -213,7 +222,7 @@ def tile_stackeddeepmixtureofexperts_x1_kernel(tc, x, wg1, w1, b1, wg2, gamma, w
 
         def relu1(k, e, eng="s"):
             i = k % NT
-            r = work.tile([P, T, P], F32, name="r", bufs=12, align_bytes=64)
+            r = work.tile([P, T, P], F32, name="r", bufs=RB, align_bytes=64)
             gate = g1[i // 2][:, i % 2, e : e + 1]
             if eng == "s":
                 nc.scalar.activation(out=r[:], in_=tt1[k, e][:], func=ACT.Relu, scale=gate)
@@ -221,19 +230,24 @@ def tile_stackeddeepmixtureofexperts_x1_kernel(tc, x, wg1, w1, b1, wg2, gamma, w
                 nc.gpsimd.tensor_scalar(out=r[:], in0=tt1[k, e][:], scalar1=gate, scalar2=0.0, op0=MUL, op1=MAX)
             r1[k, e] = r
 
-        def turn1(k):
-            z = zp.tile([P, T, P], F32, name="z")
-            for t in range(T):
-                for e in range(E):
+        def pair_add(k, e):
+            nc.gpsimd.tensor_tensor(out=r1[k, e][:], in0=r1[k, e][:], in1=r1[k, e + 1][:], op=ADD)
+
+        def turn1(k, ts):
+            if 0 in ts:
+                z = zp.tile([P, T, P], F32, name="z")
+                zps[k] = z
+            z = zps[k]
+            for t in ts:
+                for e in TE:
                     nc.tensor.matmul(
                         out=z[:, t, :],
                         lhsT=r1[k, e][:, t, :],
                         rhs=ident[:],
                         is_transpose=True,
-                        start=(e == 0),
-                        stop=(e == E - 1),
+                        start=(e == TE[0]),
+                        stop=(e == TE[-1]),
                     )
-            zps[k] = z
 
         def z_copy(k):
             zz = work.tile([P, T, P], F32, name="z1", bufs=11, align_bytes=64)
@@ -243,9 +257,11 @@ def tile_stackeddeepmixtureofexperts_x1_kernel(tc, x, wg1, w1, b1, wg2, gamma, w
         def u_mul(k):
             g = k // NT
             u = work.tile([P, P, T], BF16, name="ub", bufs=3, align_bytes=64)
-            nc.vector.tensor_tensor(
+            on_g = UG[k % len(UG)]
+            eng = nc.gpsimd if on_g else nc.vector
+            eng.tensor_tensor(
                 out=u[:],
-                in0=zps[k][:].rearrange("p t n -> p n t"),
+                in0=(z1[k] if on_g else zps[k])[:].rearrange("p t n -> p n t"),
                 in1=gam[:, g, :].unsqueeze(1).to_broadcast([P, P, T]),
                 op=MUL,
             )
@@ -260,7 +276,7 @@ def tile_stackeddeepmixtureofexperts_x1_kernel(tc, x, wg1, w1, b1, wg2, gamma, w
         lg2 = {}
 
         def logits2(i):
-            lg2[i // 2] = lgs[:, 1, i - i % 2 : i - i % 2 + 2, :]
+            lg2[i // 2] = lgs2[:, i % 4 - i % 2 : i % 4 - i % 2 + 2, :]
             for g in range(G):
                 for t in range(T):
                     nc.tensor.matmul(
@@ -343,6 +359,7 @@ def tile_stackeddeepmixtureofexperts_x1_kernel(tc, x, wg1, w1, b1, wg2, gamma, w
                 )
 
         make_identity(nc, ident[:])
+        nc.gpsimd.memset(wg2_sb[:], 0.0)
         nc.gpsimd.memset(warm[:], 0.0)
         nc.scalar.activation(out=warm[:], in_=warm[:], func=ACT.Exp)
 
@@ -364,21 +381,23 @@ def tile_stackeddeepmixtureofexperts_x1_kernel(tc, x, wg1, w1, b1, wg2, gamma, w
                 )
 
         nc.sync.dma_start(out=wg1_sb[:], in_=wg1.rearrange("(p t) e -> p t e", t=T))
-        load_x(0)
-        load_piece(pieces[0])
-        load_bias(0)
-        load_piece(pieces[1])
-        load_piece(pieces[2])
-        load_x(1)
-        load_piece(pieces[3])
-        load_x(2)
-        nc.sync.dma_start(out=gam[:], in_=gamma.rearrange("(g p t) -> p g t", g=G, t=T))
-        load_x(3)
-        nc.sync.dma_start(out=wg2_bf[:], in_=wg2.rearrange("(g p t) e -> p g t e", g=G, t=T))
-        load_piece(pieces[4])
-        load_bias(1)
-        for pc in pieces[5:8]:
-            load_piece(pc)
+        def load_gamma():
+            nc.sync.dma_start(out=gam[:], in_=gamma.rearrange("(g p t) -> p g t", g=G, t=T))
+
+        def load_wg2():
+            nc.sync.dma_start(out=wg2_bf[:], in_=wg2.rearrange("(g p t) e -> p g t e", g=G, t=T))
+
+        for kind, j in LOADS:
+            if kind == "x":
+                load_x(j)
+            elif kind == "w":
+                load_piece(pieces[j])
+            elif kind == "b":
+                load_bias(j)
+            elif kind == "g":
+                load_gamma()
+            else:
+                load_wg2()
 
         for once in range(1):
             perm_bias(0)
@@ -427,11 +446,14 @@ def tile_stackeddeepmixtureofexperts_x1_kernel(tc, x, wg1, w1, b1, wg2, gamma, w
             so[2]()
             for e in range(E):
                 mm1(2, e)
-            turn1(0)
+            for e in PA:
+                pair_add(0, e - 1)
+                pair_add(1, e - 1)
+            turn1(0, (0, 1, 2, 3))
             so[3]()
             so[4]()
             perm_bias(1)
-            nc.gpsimd.tensor_copy(out=wg2_sb[:], in_=wg2_bf[:])
+            nc.gpsimd.tensor_copy(out=wg2_sb[:, :, :, :E], in_=wg2_bf[:])
 
             state = {"loaded": 8}
 
@@ -452,69 +474,103 @@ def tile_stackeddeepmixtureofexperts_x1_kernel(tc, x, wg1, w1, b1, wg2, gamma, w
                 add2(e, i, A2[n % len(A2)])
 
             smx = []
-            for k in range(2, 20):
+            pos_of = {b: p for p, b in enumerate(seq)}
+            pair_g1_done = {}
+            gates_ready = {}
+            quant_done = [4]
+            waiting_units = [(e, i) for e in range(E) for i in range(NT)]
+            fin_queue = []
+
+            def out_steps(n_now, last=False):
+                for item in list(fin_queue):
+                    i, n0, st = item
+                    if n_now - n0 >= LG + st:
+                        if st == 0:
+                            out_turn(i)
+                        elif st == 1:
+                            out_copy(i, OC[i % len(OC)])
+                        else:
+                            out_quant(i)
+                            if i % 4 == 3:
+                                out_store(i // 4)
+                        fin_queue.remove(item)
+                        if st < 2:
+                            fin_queue.append((i, n0, st + 1))
+
+            def do_unit(e, i):
+                n = count[0]
+                unit(e, i)
+                unit_add(e, i, n)
+                if e == E - 1:
+                    fin_queue.append((i, n, 0))
+                out_steps(n)
+
+            npos = len(seq) + 3
+            for p in range(2, npos):
+                b = seq[p] if p < len(seq) else None
                 slots = [[] for q in range(E)]
-                if k in (2, 4):
-                    j = k // 2 + 1
-                    slots[0].append(lambda: x_a(j, "s"))
-                    slots[2].append(lambda: (lg1.update({j: logits1(j)}), x_quant(j)))
-                if k in (3, 5):
-                    j = (k + 1) // 2
-                    smx += softmax_ops(lg1[j], g1[j])
-                if k >= 13 and k % 2 == 1:
-                    smx += softmax_ops(lg2[(k - 13) // 2], g2[(k - 13) // 2])
+                for j in (2, 3):
+                    if p == pos_of[2 * j] - 2:
+                        slots[0].append(lambda j=j: x_a(j, XE[j]))
+                        slots[2].append(lambda j=j: (lg1.update({j: logits1(j)}), x_quant(j)))
+                    if p == pos_of[2 * j] - 1:
+                        smx += softmax_ops(lg1[j], g1[j])
+                for j in range(4):
+                    if gates_ready.get(j) == p - 1:
+                        smx += softmax_ops(lg2[j], g2[j])
                 for q in range(E):
                     if smx:
                         slots[q].insert(0, smx.pop(0))
-                if k in (3, 5):
+                if smx:
                     slots[3].insert(1, smx.pop(0))
-                if k in quant_at:
-                    slots[1].append(lambda: prep_quant(pieces[quant_at[k]]))
-                if 0 <= k - 3 < 16:
-                    slots[0].append(lambda: u_quant(k - 3))
-                if k - 2 < 16:
-                    slots[2].append(lambda: (u_mul(k - 2), z_copy(k - 2)))
-                if k in prep_at:
-                    slots[3].append(lambda: (prep_copy(pieces[prep_at[k][0]], *prep_at[k][1:]), load_next()))
+                if p in quant_at:
+                    def q_fn(p=p):
+                        for pc in quant_at[p]:
+                            prep_quant(pieces[pc])
+                            quant_done[0] = pc + 1
+                    slots[1].append(q_fn)
+                if 0 <= p - 3 < len(seq):
+                    slots[0].append(lambda: u_quant(seq[p - 3]))
+                if p - 2 < len(seq):
+                    slots[2].append(lambda: (z_copy(seq[p - 2]), u_mul(seq[p - 2])) if UG[seq[p - 2] % len(UG)] else (u_mul(seq[p - 2]), z_copy(seq[p - 2])))
+                if p in prep_at:
+                    for pr in prep_at[p]:
+                        slots[3].append(lambda pr=pr: (prep_copy(pieces[pr[0]], *pr[1:]), load_next()))
                 for e in range(E):
-                    if k < 16:
-                        add1(k, e)
-                        relu1(k, e, relu_eng(k, e))
+                    if b is not None:
+                        add1(b, e)
+                        relu1(b, e, relu_eng(b, e))
+                        if e in PA:
+                            pair_add(b, e - 1)
                     for fn in slots[e]:
                         fn()
-                if k - 1 < 16:
-                    turn1(k - 1)
-                if k + 1 < 16:
-                    for e in range(E):
-                        mm1(k + 1, e)
-                if 10 <= k < 18:
-                    logits2(k - 10)
-                for e, i in units_at.get(k, []):
-                    n = count[0]
-                    unit(e, i)
-                    unit_add(e, i, n)
+                for c in PEO:
+                    if c < E and p + 1 < len(seq):
+                        mm1(seq[p + 1], c)
+                    if c == E and p - 1 < len(seq):
+                        turn1(seq[p - 1], (0, 1, 2, 3))
+                    if c > E and p - 1 < len(seq):
+                        turn1(seq[p - 1], (0, 1) if c == E + 1 else (2, 3))
+                if p - 2 < len(seq) and seq[p - 2] >= NT:
+                    i = seq[p - 2] - NT
+                    logits2(i)
+                    if i % 2 == 1:
+                        gates_ready[i // 2] = p
+                todo = UPP[p] if p < len(UPP) else 0
+                for e, i in list(waiting_units):
+                    if todo and gates_ready.get(i // 2, 99) <= p - 2 and 8 + 2 * e + 1 < quant_done[0]:
+                        do_unit(e, i)
+                        waiting_units.remove((e, i))
+                        todo -= 1
             for fn in smx:
                 fn()
-
-            LG = 2
-            for n in range(len(tail) + 4 + LG):
-                if n in prep_tail:
-                    prep_copy(pieces[prep_tail[n][0]], prep_tail[n][1])
-                if n < len(tail):
-                    unit(*tail[n])
-                if n - 2 in prep_tail:
-                    prep_quant(pieces[prep_tail[n - 2][0]])
-                f0 = tail[n - 1] if 0 <= n - 1 < len(tail) else None
-                f1 = tail[n - 1 - LG] if 0 <= n - 1 - LG < len(tail) else (0, 0)
-                f2 = tail[n - 2 - LG] if 0 <= n - 2 - LG < len(tail) else (0, 0)
-                f3 = tail[n - 3 - LG] if 0 <= n - 3 - LG < len(tail) else (0, 0)
-                if f0 is not None:
-                    unit_add(*f0, n)
-                if f1[0] == E - 1:
-                    out_turn(f1[1])
-                if f2[0] == E - 1:
-                    out_copy(f2[1], "s" if f2[1] % 2 else "v")
-                if f3[0] == E - 1:
-                    out_quant(f3[1])
-                    if f3[1] % 4 == 3:
-                        out_store(f3[1] // 4)
+            for m, (e, i) in enumerate(waiting_units):
+                if m in prep_tail:
+                    for pr in prep_tail[m]:
+                        prep_copy(pieces[pr[0]], *pr[1:])
+                if m in quant_tail:
+                    for pc in quant_tail[m]:
+                        prep_quant(pieces[pc])
+                do_unit(e, i)
+            for m in range(LG + 4):
+                out_steps(count[0] + m)

from contextlib import ExitStack

import concourse.mybir as mybir
from concourse.masks import make_identity

N, D, F, E, O = 1024, 512, 1024, 4, 512
FLOPS = 2 * N * D * F * E + 2 * N * F * O * E

F32 = mybir.dt.float32
BF16 = mybir.dt.bfloat16
U32 = mybir.dt.uint32
I32 = mybir.dt.int32
U8 = mybir.dt.uint8
X4 = mybir.dt.float8_e4m3fn_x4
ADD = mybir.AluOpType.add
SUB = mybir.AluOpType.subtract
MUL = mybir.AluOpType.mult
MAX = mybir.AluOpType.max
AX = mybir.AxisListType.X
ACT = mybir.ActivationFunctionType

P = 128
T = 4
G = 2
NT = N // P

LOADS = [['x', 0], ['w', 0], ['b', 0], ['w', 1], ['w', 2], ['w', 3], ['x', 1], ['g', 0], ['x', 2], ['x', 3], ['h', 0], ['w', 4], ['b', 1], ['w', 5], ['w', 6], ['w', 7]]
UG = [0]
PEO = [0, 1, 4, 2, 3]
LW = 64
HC = 208
LG = 3
GPS = ()
PA = (1, 3)
TE = (0, 2)
R2 = 'sssv'
A2 = 'vg'
OC = 'vs'
XE = 'vvss'
RB = 16
MB = 4
ZB = 3
seq = [0, 1, 2, 3, 4, 5, 6, 7, 8, 9, 10, 11, 12, 13, 14, 15]
prep_at = {2: [(4, 128, 384)], 3: [(5, 128, 256)], 4: [(6, 128, 512)], 5: [(7, 128, 512)], 6: [(8, 384, 384)], 9: [(9, 256, 512), (10, 0, 256)], 12: [(11, 128, 128)], 13: [(12, 128, 512)], 15: [(13, 512, 512)], 16: [(14, 192, 512)], 17: [(15, 192, 256)]}
quant_at = {3: [4], 4: [5], 5: [6], 6: [7], 7: [8], 10: [9], 11: [10], 14: [11, 12], 16: [13], 18: [14, 15]}
prep_tail = {}
quant_tail = {}
UPP = [0, 0, 0, 0, 0, 0, 0, 0, 0, 0, 0, 2, 2, 0, 4, 0, 2, 3, 4]


def tile_stackeddeepmixtureofexperts_x1_kernel(tc, x, wg1, w1, b1, wg2, gamma, w2, out_0, out_1, out_2):
    nc = tc.nc
    with ExitStack() as ctx:
        keep = ctx.enter_context(tc.tile_pool(name="keep", bufs=1))
        work = ctx.enter_context(tc.tile_pool(name="work", bufs=3))
        mmp = ctx.enter_context(tc.psum_pool(name="mmp", bufs=MB))
        zp = ctx.enter_context(tc.psum_pool(name="zp", bufs=ZB))
        mp = ctx.enter_context(tc.psum_pool(name="mp", bufs=1))

        ident = keep.tile([P, P], F32, name="ident", align_bytes=64)
        wg1_sb = keep.tile([P, T, E], BF16, name="wg1_sb", align_bytes=64)
        wg2_bf = keep.tile([P, G, T, E], BF16, name="wg2_bf", align_bytes=64)
        wg2_sb = keep.tile([P, G, T, LW], F32, name="wg2_sb", align_bytes=64)
        gam = keep.tile([P, G, T], BF16, name="gam", align_bytes=64)
        b_raw = [keep.tile([P, E, 512], BF16, name=f"b_raw{g}", align_bytes=64) for g in range(G)]
        b_perm = [keep.tile([P, E, T, P], BF16, name=f"b_perm{g}", align_bytes=64) for g in range(G)]
        x_sb = [keep.tile([P, 2, D], BF16, name=f"x_sb{j}", align_bytes=64) for j in range(4)]
        xg = [keep.tile([P, 256, T], BF16, name=f"xg{j}", align_bytes=64) for j in range(4)]
        xc = [keep.tile([P, 256], U32, name=f"xc{j}", align_bytes=64) for j in range(4)]
        xs = [keep.tile([P, 256], U8, name=f"xs{j}", align_bytes=64) for j in range(4)]
        g1 = [keep.tile([P, 2, E], F32, name=f"g1_{j}", align_bytes=64) for j in range(4)]
        g2 = [keep.tile([P, 2, E], F32, name=f"g2_{j}", align_bytes=64) for j in range(4)]
        uc = [[keep.tile([P, P], U32, name=f"uc{g}_{i}", align_bytes=64) for i in range(NT)] for g in range(G)]
        us = [[keep.tile([P, P], U8, name=f"us{g}_{i}", align_bytes=64) for i in range(NT)] for g in range(G)]
        acc = [keep.tile([P, O], F32, name=f"acc{i}", align_bytes=64) for i in range(NT)]
        oc = [keep.tile([P, 512], U32, name=f"oc{h}", align_bytes=64) for h in range(2)]
        osc = [keep.tile([P, 512], U8, name=f"osc{h}", align_bytes=64) for h in range(2)]
        warm = keep.tile([P, 1], F32, name="warm")

        w_codes = {}
        w_scales = {}
        for s in range(2):
            for g in range(G):
                for e in range(E):
                    w_codes[s, g, e] = keep.tile([P, 512], U32, name=f"wc{s}_{g}_{e}", align_bytes=64)
                    w_scales[s, g, e] = keep.tile([P, 512], U8, name=f"ws{s}_{g}_{e}", align_bytes=64)

        lgs = mp.tile([P, NT * E + 4 * LW], F32, name="lgs")
        lgs1 = lgs[:, : NT * E].rearrange("p (i e) -> p i e", e=E)
        lgs2 = lgs[:, NT * E :].rearrange("p (i e) -> p i e", e=LW)

        pieces = [(0, 0, e) for e in range(E)] + [(0, 1, e) for e in range(E)]
        pieces += [(1, g, e) for e in range(E) for g in range(G)]

        raw = {}
        grouped = {}

        def load_piece(pc):
            s, g, e = pc
            w_raw = work.tile([P, T, 512], BF16, name="w_raw", bufs=8, align_bytes=64)
            if s == 0:
                src = w1[e, :, 512 * g : 512 * (g + 1)]
            else:
                src = w2[e, 512 * g : 512 * (g + 1), :]
            nc.sync.dma_start(out=w_raw[:], in_=src.rearrange("(p j) c -> p j c", j=T))
            raw[pc] = w_raw

        def prep_copy_g(pc, c0, n):
            for q in range(n):
                a, b = c0 + (512 - c0) * q // n, c0 + (512 - c0) * (q + 1) // n
                nc.gpsimd.tensor_scalar(
                    out=grouped[pc][:, a:b, :],
                    in0=raw[pc][:, :, a:b].rearrange("p j c -> p c j"),
                    scalar1=1.0,
                    scalar2=0.0,
                    op0=MUL,
                    op1=ADD,
                )

        def prep_copy(pc, c, cg=512):
            w_grp = work.tile([P, 512, T], BF16, name="w_grp", bufs=3, align_bytes=64)
            grouped[pc] = w_grp
            if cg < 512:
                prep_copy_g(pc, cg, 4)
            if c > 0:
                nc.vector.tensor_copy(out=w_grp[:, :c, :], in_=raw[pc][:, :, :c].rearrange("p j c -> p c j"))
            if c < cg:
                nc.scalar.copy(out=w_grp[:, c:cg, :], in_=raw[pc][:, :, c:cg].rearrange("p j c -> p c j"))

        def prep_quant(pc):
            nc.vector.quantize_mx(
                out=w_codes[pc][:].bitcast(X4),
                scales=w_scales[pc][:],
                in_=grouped[pc][:].rearrange("p c j -> p (c j)"),
            )

        def x_turn(j):
            xt = mmp.tile([P, 2, 2, P], F32, name="ps")
            for i in range(2):
                words = x_sb[j][:, i, :].bitcast(F32)
                for u in range(2):
                    nc.tensor.transpose(xt[:, i, u, :], words[:, u:256:2], ident[:])
            return xt

        def x_copy(j, xt, eng):
            dst = xg[j][:].rearrange("p n t -> p (n t)").bitcast(F32).rearrange("p (i r u) -> p i r u", i=2, u=2)
            src = xt[:].rearrange("p i u r -> p i r u")
            if eng == "v":
                nc.vector.tensor_copy(out=dst, in_=src)
            else:
                nc.scalar.copy(out=dst, in_=src)

        def x_quant(j):
            nc.vector.quantize_mx(out=xc[j][:].bitcast(X4), scales=xs[j][:], in_=xg[j][:].rearrange("p n t -> p (n t)"))

        def logits1(j):
            lg = lgs1[:, 2 * j : 2 * j + 2, :]
            for i in range(2):
                for t in range(T):
                    nc.tensor.matmul(
                        out=lg[:, i, :],
                        lhsT=xg[j][:, P * i : P * (i + 1), t],
                        rhs=wg1_sb[:, t, :],
                        start=(t == 0),
                        stop=(t == T - 1),
                    )
            return lg

        def softmax_ops(lg, gt):
            mx = work.tile([P, 2], F32, name="mx", align_bytes=64)
            dl = work.tile([P, 2, E], F32, name="dl", align_bytes=64)
            ex = work.tile([P, 2, E], F32, name="ex", align_bytes=64)
            sm = work.tile([P, 2], F32, name="sm", align_bytes=64)
            rc = work.tile([P, 2], F32, name="rc", align_bytes=64)

            def top():
                nc.vector.tensor_reduce(out=mx[:], in_=lg[:, :, :E], axis=AX, op=MAX)

            def exps():
                nc.vector.tensor_tensor(out=dl[:], in0=lg[:, :, :E], in1=mx[:].unsqueeze(2).to_broadcast([P, 2, E]), op=SUB)
                nc.scalar.activation(out=ex[:], in_=dl[:], func=ACT.Exp)

            def total():
                nc.vector.tensor_reduce(out=sm[:], in_=ex[:], axis=AX, op=ADD)

            def inverse():
                nc.vector.reciprocal(out=rc[:], in_=sm[:])

            def gates():
                nc.vector.tensor_tensor(out=gt[:], in0=ex[:], in1=rc[:].unsqueeze(2).to_broadcast([P, 2, E]), op=MUL)

            return [top, exps, total, inverse, gates]

        ps1 = {}
        tt1 = {}
        r1 = {}
        zps = {}
        z1 = {}
        ub = {}

        def mm1(k, e):
            g, i = divmod(k, NT)
            cols = slice(P * (i % 2), P * (i % 2 + 1))
            ps = mmp.tile([P, 512], F32, name="ps")
            nc.tensor.matmul_mx(
                out=ps[:],
                lhsT=xc[i // 2][:, cols].bitcast(X4),
                lhsT_scale=xs[i // 2][:, cols],
                rhs=w_codes[0, g, e][:].bitcast(X4),
                rhs_scale=w_scales[0, g, e][:],
                start=True,
                stop=True,
            )
            ps1[k, e] = ps

        def add1(k, e):
            tt = work.tile([P, T, P], F32, name="tt", bufs=4, align_bytes=64)
            nc.vector.tensor_tensor(
                out=tt[:], in0=ps1[k, e][:].rearrange("p (m t) -> p t m", t=T), in1=b_perm[k // NT][:, e], op=ADD
            )
            tt1[k, e] = tt

        def relu1(k, e, eng="s"):
            i = k % NT
            r = work.tile([P, T, P], F32, name="r", bufs=RB, align_bytes=64)
            gate = g1[i // 2][:, i % 2, e : e + 1]
            if eng == "s":
                nc.scalar.activation(out=r[:], in_=tt1[k, e][:], func=ACT.Relu, scale=gate)
            else:
                nc.gpsimd.tensor_scalar(out=r[:], in0=tt1[k, e][:], scalar1=gate, scalar2=0.0, op0=MUL, op1=MAX)
            r1[k, e] = r

        def pair_add(k, e):
            nc.gpsimd.tensor_tensor(out=r1[k, e][:], in0=r1[k, e][:], in1=r1[k, e + 1][:], op=ADD)

        def turn1(k, ts):
            if 0 in ts:
                z = zp.tile([P, T, P], F32, name="z")
                zps[k] = z
            z = zps[k]
            for t in ts:
                for e in TE:
                    nc.tensor.matmul(
                        out=z[:, t, :],
                        lhsT=r1[k, e][:, t, :],
                        rhs=ident[:],
                        is_transpose=True,
                        start=(e == TE[0]),
                        stop=(e == TE[-1]),
                    )

        def z_copy(k):
            zz = work.tile([P, T, P], F32, name="z1", bufs=11, align_bytes=64)
            nc.scalar.copy(out=zz[:], in_=zps[k][:])
            z1[k] = zz

        def u_mul(k):
            g = k // NT
            u = work.tile([P, P, T], BF16, name="ub", bufs=3, align_bytes=64)
            on_g = UG[k % len(UG)]
            eng = nc.gpsimd if on_g else nc.vector
            eng.tensor_tensor(
                out=u[:],
                in0=(z1[k] if on_g else zps[k])[:].rearrange("p t n -> p n t"),
                in1=gam[:, g, :].unsqueeze(1).to_broadcast([P, P, T]),
                op=MUL,
            )
            ub[k] = u

        def u_quant(k):
            g, i = divmod(k, NT)
            nc.vector.quantize_mx(
                out=uc[g][i][:].bitcast(X4), scales=us[g][i][:], in_=ub[k][:].rearrange("p n t -> p (n t)")
            )

        lg2 = {}

        def logits2(i):
            lg2[i // 2] = lgs2[:, i % 4 - i % 2 : i % 4 - i % 2 + 2, :]
            for g in range(G):
                for t in range(T):
                    nc.tensor.matmul(
                        out=lg2[i // 2][:, i % 2, :],
                        lhsT=z1[NT * g + i][:, t, :],
                        rhs=wg2_sb[:, g, t, :],
                        start=(g == 0 and t == 0),
                        stop=(g == G - 1 and t == T - 1),
                    )

        ps2 = {}
        r2 = {}

        def mm2(e, i):
            q = mmp.tile([P, 512], F32, name="ps")
            for g in range(G):
                nc.tensor.matmul_mx(
                    out=q[:],
                    lhsT=uc[g][i][:].bitcast(X4),
                    lhsT_scale=us[g][i][:],
                    rhs=w_codes[1, g, e][:].bitcast(X4),
                    rhs_scale=w_scales[1, g, e][:],
                    start=(g == 0),
                    stop=(g == G - 1),
                )
            ps2[e, i] = q

        def relu2(e, i, eng):
            gate = g2[i // 2][:, i % 2, e : e + 1]
            if e == 0:
                dst = acc[i]
            else:
                rr = work.tile([P, O], F32, name="rr", bufs=5, align_bytes=64)
                dst = rr
            r2[e, i] = dst
            if eng == "s":
                nc.scalar.activation(out=dst[:], in_=ps2[e, i][:], func=ACT.Relu, scale=gate)
            else:
                nc.vector.tensor_scalar(out=dst[:], in0=ps2[e, i][:], scalar1=gate, scalar2=0.0, op0=MUL, op1=MAX)

        def add2(e, i, eng):
            if e == 0:
                return
            e_ = nc.gpsimd if eng == "g" else nc.vector
            e_.tensor_tensor(out=acc[i][:], in0=acc[i][:], in1=r2[e, i][:], op=ADD)

        ot = {}
        pb = {}

        def out_turn(i):
            nc.sync.dma_start(out=out_0[P * i : P * (i + 1), :], in_=acc[i][:])
            z = zp.tile([P, T, P], F32, name="z")
            for t in range(T):
                nc.tensor.transpose(z[:, t, :], acc[i][:, t:O:T], ident[:])
            ot[i] = z

        def out_copy(i, eng):
            b = work.tile([P, P, T], BF16, name="pb", bufs=3, align_bytes=64)
            src = ot[i][:].rearrange("p t n -> p n t")
            if eng == "s":
                nc.scalar.copy(out=b[:], in_=src)
            else:
                nc.vector.tensor_copy(out=b[:], in_=src)
            pb[i] = b

        def out_quant(i):
            h, c = divmod(i, 4)
            cols = slice(P * c, P * (c + 1))
            nc.vector.quantize_mx(
                out=oc[h][:, cols].bitcast(X4), scales=osc[h][:, cols], in_=pb[i][:].rearrange("p n t -> p (n t)")
            )

        def out_store(h):
            words = out_1[0].rearrange("p m t -> p (m t)")
            nc.sync.dma_start(out=words[:, 2048 * h : 2048 * (h + 1)].bitcast(I32), in_=oc[h][:].bitcast(I32))
            for q in range(4):
                nc.sync.dma_start(
                    out=out_2[0, 4 * q : 4 * q + 4, 512 * h : 512 * (h + 1)].bitcast(I32),
                    in_=osc[h][32 * q : 32 * q + 4, :].bitcast(I32),
                )

        make_identity(nc, ident[:])
        nc.gpsimd.memset(wg2_sb[:], 0.0)
        nc.gpsimd.memset(warm[:], 0.0)
        nc.scalar.activation(out=warm[:], in_=warm[:], func=ACT.Exp)

        def load_x(j):
            nc.sync.dma_start(out=x_sb[j][:], in_=x[256 * j : 256 * (j + 1), :].rearrange("(i p) k -> p i k", p=P))

        def load_bias(g):
            nc.sync.dma_start(out=b_raw[g][:], in_=b1[:, 512 * g : 512 * (g + 1)].partition_broadcast(P))

        def perm_bias(g):
            for e in range(E):
                nc.gpsimd.tensor_scalar(
                    out=b_perm[g][:, e],
                    in0=b_raw[g][:, e, :].rearrange("p (m t) -> p t m", t=T),
                    scalar1=1.0,
                    scalar2=0.0,
                    op0=MUL,
                    op1=ADD,
                )

        nc.sync.dma_start(out=wg1_sb[:], in_=wg1.rearrange("(p t) e -> p t e", t=T))
        def load_gamma():
            nc.sync.dma_start(out=gam[:], in_=gamma.rearrange("(g p t) -> p g t", g=G, t=T))

        def load_wg2():
            nc.sync.dma_start(out=wg2_bf[:], in_=wg2.rearrange("(g p t) e -> p g t e", g=G, t=T))

        for kind, j in LOADS:
            if kind == "x":
                load_x(j)
            elif kind == "w":
                load_piece(pieces[j])
            elif kind == "b":
                load_bias(j)
            elif kind == "g":
                load_gamma()
            else:
                load_wg2()

        for once in range(1):
            perm_bias(0)

            def x_a(j, eng):
                xt = x_turn(j)
                x_copy(j, xt, eng)

            lg1 = {}

            def relu_eng(k, e):
                return "g" if e in GPS else "s"

            x_a(0, "v")
            lg1[0] = logits1(0)
            prep_copy(pieces[0], HC)
            x_quant(0)
            so = softmax_ops(lg1[0], g1[0])
            so[0]()
            so[1]()
            prep_copy(pieces[1], HC)
            prep_quant(pieces[0])
            so[2]()
            so[3]()
            so[4]()
            for e in range(E):
                mm1(0, e)
                mm1(1, e)
                if e + 2 < E:
                    prep_copy(pieces[e + 2], HC)
                add1(0, e)
                relu1(0, e, relu_eng(0, e))
                if e + 1 < E:
                    prep_quant(pieces[e + 1])
                add1(1, e)
                relu1(1, e, relu_eng(1, e))
                if e == 0:
                    x_a(1, "v")
                if e == 1:
                    lg1[1] = logits1(1)
                    x_quant(1)
                    so = softmax_ops(lg1[1], g1[1])
                if e == 2:
                    so[0]()
                    so[1]()
            so[2]()
            for e in range(E):
                mm1(2, e)
            for e in PA:
                pair_add(0, e - 1)
                pair_add(1, e - 1)
            turn1(0, (0, 1, 2, 3))
            so[3]()
            so[4]()
            perm_bias(1)
            nc.gpsimd.tensor_copy(out=wg2_sb[:, :, :, :E], in_=wg2_bf[:])

            state = {"loaded": 8}

            def load_next():
                if state["loaded"] < len(pieces):
                    load_piece(pieces[state["loaded"]])
                    state["loaded"] += 1

            count = [0]

            def unit(e, i):
                n = count[0]
                mm2(e, i)
                relu2(e, i, R2[n % len(R2)])
                count[0] += 1

            def unit_add(e, i, n):
                add2(e, i, A2[n % len(A2)])

            smx = []
            pos_of = {b: p for p, b in enumerate(seq)}
            pair_g1_done = {}
            gates_ready = {}
            quant_done = [4]
            waiting_units = [(e, i) for e in range(E) for i in range(NT)]
            fin_queue = []

            def out_steps(n_now, last=False):
                for item in list(fin_queue):
                    i, n0, st = item
                    if n_now - n0 >= LG + st:
                        if st == 0:
                            out_turn(i)
                        elif st == 1:
                            out_copy(i, OC[i % len(OC)])
                        else:
                            out_quant(i)
                            if i % 4 == 3:
                                out_store(i // 4)
                        fin_queue.remove(item)
                        if st < 2:
                            fin_queue.append((i, n0, st + 1))

            def do_unit(e, i):
                n = count[0]
                unit(e, i)
                unit_add(e, i, n)
                if e == E - 1:
                    fin_queue.append((i, n, 0))
                out_steps(n)

            npos = len(seq) + 3
            for p in range(2, npos):
                b = seq[p] if p < len(seq) else None
                slots = [[] for q in range(E)]
                for j in (2, 3):
                    if p == pos_of[2 * j] - 2:
                        slots[0].append(lambda j=j: x_a(j, XE[j]))
                        slots[2].append(lambda j=j: (lg1.update({j: logits1(j)}), x_quant(j)))
                    if p == pos_of[2 * j] - 1:
                        smx += softmax_ops(lg1[j], g1[j])
                for j in range(4):
                    if gates_ready.get(j) == p - 1:
                        smx += softmax_ops(lg2[j], g2[j])
                for q in range(E):
                    if smx:
                        slots[q].insert(0, smx.pop(0))
                if smx:
                    slots[3].insert(1, smx.pop(0))
                if p in quant_at:
                    def q_fn(p=p):
                        for pc in quant_at[p]:
                            prep_quant(pieces[pc])
                            quant_done[0] = pc + 1
                    slots[1].append(q_fn)
                if 0 <= p - 3 < len(seq):
                    slots[0].append(lambda: u_quant(seq[p - 3]))
                if p - 2 < len(seq):
                    slots[2].append(lambda: (z_copy(seq[p - 2]), u_mul(seq[p - 2])) if UG[seq[p - 2] % len(UG)] else (u_mul(seq[p - 2]), z_copy(seq[p - 2])))
                if p in prep_at:
                    for pr in prep_at[p]:
                        slots[3].append(lambda pr=pr: (prep_copy(pieces[pr[0]], *pr[1:]), load_next()))
                for e in range(E):
                    if b is not None:
                        add1(b, e)
                        relu1(b, e, relu_eng(b, e))
                        if e in PA:
                            pair_add(b, e - 1)
                    for fn in slots[e]:
                        fn()
                for c in PEO:
                    if c < E and p + 1 < len(seq):
                        mm1(seq[p + 1], c)
                    if c == E and p - 1 < len(seq):
                        turn1(seq[p - 1], (0, 1, 2, 3))
                    if c > E and p - 1 < len(seq):
                        turn1(seq[p - 1], (0, 1) if c == E + 1 else (2, 3))
                if p - 2 < len(seq) and seq[p - 2] >= NT:
                    i = seq[p - 2] - NT
                    logits2(i)
                    if i % 2 == 1:
                        gates_ready[i // 2] = p
                todo = UPP[p] if p < len(UPP) else 0
                for e, i in list(waiting_units):
                    if todo and gates_ready.get(i // 2, 99) <= p - 2 and 8 + 2 * e + 1 < quant_done[0]:
                        do_unit(e, i)
                        waiting_units.remove((e, i))
                        todo -= 1
            for fn in smx:
                fn()
            for m, (e, i) in enumerate(waiting_units):
                if m in prep_tail:
                    for pr in prep_tail[m]:
                        prep_copy(pieces[pr[0]], *pr[1:])
                if m in quant_tail:
                    for pc in quant_tail[m]:
                        prep_quant(pieces[pc])
                do_unit(e, i)
            for m in range(LG + 4):
                out_steps(count[0] + m)
